import numpy as np
import ml_dtypes


def mxq(x, axis, fmt="e4m3"):
    dtype, down = {"e4m3": (ml_dtypes.float8_e4m3fn, 7), "e5m2": (ml_dtypes.float8_e5m2, 14)}[fmt]
    v = np.moveaxis(np.asarray(x, np.float32).astype(ml_dtypes.bfloat16).astype(np.float64), axis, -1)
    blocks = v.reshape(v.shape[:-1] + (-1, 32))
    amax = np.abs(blocks).max(-1, keepdims=True)
    byte = np.maximum(np.where(amax > 0, np.frexp(amax)[1] - 1 + 127, 0) - down, 1)
    scale = np.exp2(byte - 127.0)
    codes = (blocks / scale).astype(np.float32).astype(dtype).astype(np.float64)
    return np.moveaxis((codes * scale).reshape(v.shape), -1, axis)


WIDE = False


def mx_kscale(k):
    if not WIDE:
        return np.ones(k)
    levels = np.array([10, -10, 5, -5, 0])
    if k % 512:
        return np.exp2(np.random.permutation(np.resize(levels, k // 32))).repeat(32)
    a = np.empty((k // 512, 16))
    for p in range(k // 512):
        a[p, :8] = np.random.permutation(np.resize(levels, 8))
        for g in range(8):
            far = levels[np.abs(levels - a[p, g]) >= 10]
            a[p, g + 8] = far[np.random.randint(len(far))]
    return np.exp2(a.ravel()).repeat(32)


def f64(x):
    return np.asarray(x).astype(np.float64)


def striped(idx):
    return np.tile(np.asarray(idx).reshape(-1, 16).T, (8, 1)).astype(np.uint16)


def unstriped(offs):
    return offs[:16].T.reshape(-1).astype(np.int64)


E2M1 = np.array([0.0, 0.5, 1.0, 1.5, 2.0, 3.0, 4.0, 6.0, -0.0, -0.5, -1.0, -1.5, -2.0, -3.0, -4.0, -6.0])


def pack_weight(w, fmt):
    k, n = w.shape
    w = f64(np.asarray(w, np.float32).astype(ml_dtypes.bfloat16)).reshape(k // 32, 32, n)
    amax = np.abs(w).max(1)
    if fmt == "e4m3":
        byte = np.frexp(amax)[1] - 1 + 127 - 7
    else:
        mant, ex = np.frexp(amax / 6.0)
        byte = np.where(mant > 0.5, ex, ex - 1) + 127
    byte = np.clip(np.where(amax > 0, byte, 1), 1, 254)
    scaled = (w * np.exp2(127.0 - byte)[:, None, :]).reshape(k, n).astype(np.float32)
    by_word = np.ascontiguousarray(scaled.reshape(k // 512, 128, 4, n).transpose(0, 1, 3, 2))
    if fmt == "e4m3":
        words = by_word.astype(ml_dtypes.float8_e4m3fn).view(np.uint8)
    else:
        c = by_word.astype(ml_dtypes.float4_e2m1fn).view(np.uint8) & 0xF
        words = (c[..., 0::2] | (c[..., 1::2] << 4)).reshape(k // 512, 128, 2 * n)
    return np.ascontiguousarray(words), np.ascontiguousarray(byte.astype(np.uint8).reshape(k // 512, 16, n))


def unpack_weight(words, scales, fmt):
    g, _, n = scales.shape
    words = np.ascontiguousarray(words).reshape(g, 128, n, -1)
    if fmt == "e4m3":
        vals = words.view(ml_dtypes.float8_e4m3fn).astype(np.float64)
    else:
        nib = np.empty((g, 128, n, 4), np.uint8)
        nib[..., 0::2] = words & 0xF
        nib[..., 1::2] = words >> 4
        vals = E2M1[nib]
    vals = vals * np.repeat(np.exp2(scales.astype(np.float64) - 127.0), 8, axis=1)[..., None]
    return vals.transpose(0, 1, 3, 2).reshape(g * 512, n)


D, K, R, T, I, Q = 512, 512, 512, 2048, 512, 128


def setup_inputs():
    n = np.random.standard_normal
    idx = np.random.permutation(T)[:I]
    fd = mx_kscale(D)
    fk = mx_kscale(K)
    fr = mx_kscale(R)
    keysp = pack_weight(n((D, T)) / fd[:, None], "e4m3")
    tabp = pack_weight(n((K, T)) / fk[:, None], "e4m3")
    return {
        "query": (n((D, Q)) * 0.7 / np.sqrt(D) * fd[:, None]).astype(np.float32),
        "keys_words": keysp[0],
        "keys_scales": keysp[1],
        "tab_words": tabp[0],
        "tab_scales": tabp[1],
        "w1": (n((K, R)) * 1 / np.sqrt(K) * fk[:, None]).astype(np.float32),
        "gain": (np.random.uniform(0.5, 2.0, (R, 1))).astype(np.float32),
        "gout": (n((R, Q)) * 1 / np.sqrt(R) * fr[:, None]).astype(np.float32),
        "hsc": (np.random.uniform(0.7, 1.4, (R, 1)) / fr[:, None]).astype(np.float32),
        "old": (0.5 * n((Q, T))).astype(np.float32),
        "offs": striped(idx),
    }


def reference(query, keys_words, keys_scales, tab_words, tab_scales, w1, gain, gout, hsc, old, offs):
    idx = unstriped(offs)
    keysu = unpack_weight(keys_words, keys_scales, "e4m3")
    tabu = unpack_weight(tab_words, tab_scales, "e4m3")
    queryq = mxq(f64(query), 0, "e4m3")
    keysidxg = keysu[:, idx]
    a = queryq.T @ keysidxg
    p = np.exp(a - np.max(a, axis=1, keepdims=True))
    z = np.sum(p, axis=1, keepdims=True)
    w1q = mxq(f64(w1), 0, "e4m3")
    tabidxg = tabu[:, idx]
    zh = w1q.T @ tabidxg
    ht = np.tanh(zh)
    hv = ht * f64(gain)
    hs1 = hv * f64(hsc)
    goutq = mxq(f64(gout), 0, "e4m3")
    hs1q = mxq(hs1, 0, "e4m3")
    c0 = goutq.T @ hs1q
    dz = np.sum(c0 * p / np.square(z) * (-1.0), axis=1, keepdims=True)
    dp = c0 / z + dz
    da = dp * p
    gs = da * 512.0
    gf = np.zeros((Q, T))
    gf[:, idx] = gs
    y = f64(old) + gf
    return y

@@ -1,0 +1,213 @@
+from contextlib import ExitStack
+
+import concourse.mybir as mybir
+
+D, K, R, T, I, Q = 512, 512, 512, 2048, 512, 128
+FLOPS = 2 * (D * Q * I + K * R * I + R * Q * I)
+
+F32 = mybir.dt.float32
+BF16 = mybir.dt.bfloat16
+I32 = mybir.dt.int32
+U32 = mybir.dt.uint32
+U16 = mybir.dt.uint16
+U8 = mybir.dt.uint8
+FP8X4 = mybir.dt.float8_e4m3fn_x4
+ALU = mybir.AluOpType
+ACT = mybir.ActivationFunctionType
+AXIS = mybir.AxisListType
+
+P = 128
+PACK = 4
+CHUNK = 128
+HALF = I // 2
+STORE_WIDTHS = (256, 512, 512, 512, 256)
+
+
+def tile_attend_blrgained_soft_kernel(
+    tc, query, keys_words, keys_scales, tab_words, tab_scales, w1, gain, gout, hsc, old, offs, out
+):
+    nc = tc.nc
+
+    with ExitStack() as ctx:
+        sb = ctx.enter_context(tc.tile_pool(name="sb", bufs=1))
+        reuse = ctx.enter_context(tc.tile_pool(name="reuse", bufs=1))
+        psum = ctx.enter_context(tc.psum_pool(name="psum", bufs=1))
+
+        def tile(name, shape, dtype, tag=None):
+            return sb.tile(shape, dtype, name=name, tag=tag or name, align_bytes=64)
+
+        offsets = tile("offsets", [P, I // 16], U16)
+        tab_pool = tile("tab_pool", [P, T], U32)
+        tab_plane = reuse.tile([P, T], U8, name="tab_plane", offset=0)
+        keys_plane = tile("keys_plane", [P, T], U8)
+        w1_raw = tile("w1_raw", [P, PACK, R], F32)
+        window = tile("window", [P, T], F32)
+        factors = tile("factors", [P, 2], F32)
+        warm = tile("warm", [P, 1], F32)
+
+        nc.vector.memset(tab_plane[:].bitcast(I32), 0)
+        nc.gpsimd.memset(keys_plane[:].bitcast(I32), 0)
+        nc.vector.memset(factors[:, 0:1], 512.0)
+        nc.vector.memset(factors[:, 1:2], -1.0)
+        nc.vector.memset(window[:], 0.0)
+
+        def load_words(pool_tile, words):
+            nc.sync.dma_start(pool_tile[:].bitcast(I32), words[0].rearrange("p n t -> p (n t)").bitcast(I32))
+
+        def load_plane(queues, plane, scales):
+            rows = scales[0].bitcast(I32)
+            for f, queue in enumerate(queues):
+                queue.dma_start(plane[f:P:32, :].bitcast(I32), rows[f:16:4, :])
+
+        def load_rows(raw, matrix):
+            nc.sync.dma_start(raw[:], matrix.rearrange("(p j) w -> p j w", j=PACK))
+
+        nc.sync.dma_start(offsets[:], offs)
+        load_plane([nc.scalar] * 4, tab_plane, tab_scales)
+        load_rows(w1_raw, w1)
+        load_words(tab_pool, tab_words)
+        load_plane([nc.gpsimd] * 3 + [nc.scalar], keys_plane, keys_scales)
+
+        nc.scalar.activation(warm[:], factors[:, 1:2], ACT.Exp)
+
+        def quantize(name, grouped, width):
+            codes = tile(name + "_codes", [P, width], U32)
+            scales = tile(name + "_scales", [P, width], U8)
+            nc.vector.quantize_mx(out=codes[:].bitcast(FP8X4), scales=scales[:], in_=grouped)
+            return codes, scales
+
+        tab_bytes = tile("tab_bytes", [P, I], U8)
+        nc.vector.tensor_copy(tab_bytes[:], tab_plane[:].indirect(offsets[:]))
+        gain_sb = reuse.tile([P, PACK], F32, name="gain_sb", offset=0)
+        hsc_sb = reuse.tile([P, PACK], F32, name="hsc_sb", offset=64)
+        keys_pool = reuse.tile([P, T], U32, name="keys_pool", offset=128)
+        load_words(keys_pool, keys_words)
+        nc.gpsimd.dma_start(gain_sb[:], gain.rearrange("(p j) o -> p (j o)", j=PACK))
+        nc.gpsimd.dma_start(hsc_sb[:], hsc.rearrange("(p j) o -> p (j o)", j=PACK))
+
+        w1_dealt = w1_raw[:].rearrange("p j (m t) -> p m j t", t=PACK)
+        w1_q = []
+        for h, copy in enumerate((nc.vector.tensor_copy, nc.scalar.copy)):
+            grouped = tile("w1_bf%d" % h, [P, 2, P, PACK], BF16)
+            copy(grouped[:].rearrange("p t m j -> p m j t"), w1_dealt[:, :, :, 2 * h : 2 * h + 2])
+            w1_q.append(grouped)
+        query_raw = tile("query_raw", [P, PACK, Q], F32, tag="w1_raw")
+        load_rows(query_raw, query)
+        w1_q[0] = quantize("w1_0", w1_q[0][:].rearrange("p t m j -> p (t m j)"), 2 * P)
+        keys_bytes = tile("keys_bytes", [P, I], U8, tag="w1_bf0")
+        nc.vector.tensor_copy(keys_bytes[:], keys_plane[:].indirect(offsets[:]))
+        w1_q[1] = quantize("w1_1", w1_q[1][:].rearrange("p t m j -> p (t m j)"), 2 * P)
+        gout_raw = tile("gout_raw", [P, PACK, Q], F32, tag="keys_plane")
+        load_rows(gout_raw, gout)
+
+        def interleave(name, raw):
+            grouped = tile(name + "_bf", [P, Q, PACK], BF16)
+            nc.scalar.copy(
+                grouped[:].rearrange("p (c i) j -> p c j i", i=4),
+                raw[:].rearrange("p j (c i) -> p c j i", i=4),
+            )
+            return grouped[:].rearrange("p w j -> p (w j)")
+
+        scale_r = tile("scale_r", [P, PACK], F32)
+        nc.gpsimd.tensor_tensor(scale_r[:], gain_sb[:], hsc_sb[:], ALU.mult)
+        scale_along_slots = scale_r[:].rearrange("p (o t) -> p o t", o=1).to_broadcast([P, CHUNK, PACK])
+
+        tab_codes = []
+        for h in range(2):
+            gathered = tile("tab_codes%d" % h, [P, HALF], U32)
+            nc.vector.tensor_copy(gathered[:], tab_pool[:].indirect(offsets[:, 16 * h : 16 * (h + 1)]))
+            tab_codes.append(gathered)
+        old_sb = tile("old_sb", [P, T], F32, tag="tab_pool")
+        nc.sync.dma_start(old_sb[:], old)
+
+        ht = []
+        for c in range(I // CHUNK):
+            zh = psum.tile([P, PACK, CHUNK], F32, name="zh%d" % c)
+            first = (c * CHUNK) % HALF
+            for t in range(PACK):
+                codes, scales = w1_q[t // 2]
+                cols = slice((t % 2) * P, (t % 2 + 1) * P)
+                nc.tensor.matmul_mx(
+                    out=zh[:, t, :],
+                    lhsT=codes[:, cols].bitcast(FP8X4),
+                    lhsT_scale=scales[:, cols],
+                    rhs=tab_codes[c * CHUNK // HALF][:, first : first + CHUNK].bitcast(FP8X4),
+                    rhs_scale=tab_bytes[:, c * CHUNK : (c + 1) * CHUNK],
+                    start=True,
+                    stop=True,
+                )
+            ht_c = tile("ht%d" % c, [P, CHUNK, PACK], F32)
+            nc.scalar.activation(ht_c[:], zh[:].rearrange("p t n -> p n t"), ACT.Tanh)
+            ht.append(ht_c)
+
+        query_bf = interleave("query", query_raw)
+        gout_bf = interleave("gout", gout_raw)
+
+        c0 = psum.tile([P, I], F32, name="c0")
+        hs1_bf = {}
+        hs1_q = {}
+
+        def scale_chunk(c):
+            hs1_bf[c] = tile("hs1_bf%d" % c, [P, CHUNK, PACK], BF16)
+            nc.vector.tensor_tensor(hs1_bf[c][:], ht[c][:], scale_along_slots, ALU.mult)
+
+        def quantize_chunk(c):
+            hs1_q[c] = quantize("hs1_%d" % c, hs1_bf[c][:].rearrange("p n t -> p (n t)"), CHUNK)
+
+        scale_chunk(0)
+        scale_chunk(1)
+        quantize_chunk(0)
+        keys_codes = tile("keys_codes", [P, I], U32)
+        nc.vector.tensor_copy(keys_codes[:], keys_pool[:].indirect(offsets[:]))
+        query_codes, query_scales = quantize("query", query_bf, Q)
+        a = psum.tile([P, I], F32, name="a")
+        nc.tensor.matmul_mx(
+            out=a[:],
+            lhsT=query_codes[:].bitcast(FP8X4),
+            lhsT_scale=query_scales[:],
+            rhs=keys_codes[:].bitcast(FP8X4),
+            rhs_scale=keys_bytes[:],
+            start=True,
+            stop=True,
+        )
+        quantize_chunk(1)
+        scale_chunk(2)
+        neg_max = tile("neg_max", [P, 1], F32)
+        nc.vector.tensor_reduce(neg_max[:], a[:], AXIS.X, ALU.max, negate=True)
+        p = tile("p", [P, I], F32)
+        z = tile("z", [P, 1], F32)
+        nc.scalar.activation(p[:], a[:], ACT.Exp, bias=neg_max[:], accum_out=z[:])
+        gout_codes, gout_scales = quantize("gout", gout_bf, Q)
+        scale_chunk(3)
+        quantize_chunk(2)
+        quantize_chunk(3)
+        for c in range(I // CHUNK):
+            codes, scales = hs1_q[c]
+            nc.tensor.matmul_mx(
+                out=c0[:, c * CHUNK : (c + 1) * CHUNK],
+                lhsT=gout_codes[:].bitcast(FP8X4),
+                lhsT_scale=gout_scales[:],
+                rhs=codes[:].bitcast(FP8X4),
+                rhs_scale=scales[:],
+                start=True,
+                stop=True,
+            )
+
+        over_z = tile("over_z", [P, 1], F32)
+        nc.vector.reciprocal(over_z[:], z[:])
+        row = tile("row", [P, 2], F32)
+        nc.vector.tensor_scalar(row[:], factors[:], over_z[:], None, ALU.mult)
+
+        direct = tile("direct", [P, I], F32)
+        total = tile("total", [P, 1], F32)
+        nc.vector.scalar_tensor_tensor(direct[:], c0[:], row[:, 0:1], p[:], ALU.mult, ALU.mult, accum_out=total[:])
+        through_z = tile("through_z", [P, I], F32)
+        nc.vector.tensor_scalar(through_z[:], p[:], total[:], row[:, 1:2], ALU.mult, ALU.mult)
+        nc.vector.tensor_tensor(window[:].indirect(offsets[:]), direct[:], through_z[:], ALU.add)
+
+        first = 0
+        for width in STORE_WIDTHS:
+            cols = slice(first, first + width)
+            nc.vector.tensor_tensor(old_sb[:, cols], window[:, cols], old_sb[:, cols], ALU.add)
+            nc.sync.dma_start(out[:, cols], old_sb[:, cols])
+            first += width

@@ -20,6 +20,7 @@ P = 128
 PACK = 4
 CHUNK = 128
 HALF = I // 2
+KEYS_ROW = 4
 STORE_WIDTHS = (256, 512, 512, 512, 256)
 
 
@@ -30,7 +31,6 @@ def tile_attend_blrgained_soft_kernel(
 
     with ExitStack() as ctx:
         sb = ctx.enter_context(tc.tile_pool(name="sb", bufs=1))
-        reuse = ctx.enter_context(tc.tile_pool(name="reuse", bufs=1))
         psum = ctx.enter_context(tc.psum_pool(name="psum", bufs=1))
 
         def tile(name, shape, dtype, tag=None):
@@ -38,67 +38,65 @@ def tile_attend_blrgained_soft_kernel(
 
         offsets = tile("offsets", [P, I // 16], U16)
         tab_pool = tile("tab_pool", [P, T], U32)
-        tab_plane = reuse.tile([P, T], U8, name="tab_plane", offset=0)
+        keys_pool = tile("keys_pool", [P, T], U32)
+        tab_plane = tile("tab_plane", [P, T], U8)
         keys_plane = tile("keys_plane", [P, T], U8)
         w1_raw = tile("w1_raw", [P, PACK, R], F32)
+        query_raw = tile("query_raw", [P, PACK, Q], F32)
+        gout_raw = tile("gout_raw", [P, PACK, Q], F32)
+        gain_sb = tile("gain_sb", [P, PACK], F32)
+        hsc_sb = tile("hsc_sb", [P, PACK], F32)
+        old_sb = tile("old_sb", [P, T], F32)
         window = tile("window", [P, T], F32)
         factors = tile("factors", [P, 2], F32)
         warm = tile("warm", [P, 1], F32)
 
         nc.vector.memset(tab_plane[:].bitcast(I32), 0)
-        nc.gpsimd.memset(keys_plane[:].bitcast(I32), 0)
+        nc.vector.memset(keys_plane[:].bitcast(I32), 0)
         nc.vector.memset(factors[:, 0:1], 512.0)
         nc.vector.memset(factors[:, 1:2], -1.0)
-        nc.vector.memset(window[:], 0.0)
+        nc.gpsimd.memset(window[:], 0.0)
 
         def load_words(pool_tile, words):
             nc.sync.dma_start(pool_tile[:].bitcast(I32), words[0].rearrange("p n t -> p (n t)").bitcast(I32))
 
-        def load_plane(queues, plane, scales):
+        def load_plane(plane, first_row, scales):
             rows = scales[0].bitcast(I32)
-            for f, queue in enumerate(queues):
-                queue.dma_start(plane[f:P:32, :].bitcast(I32), rows[f:16:4, :])
+            for f in range(4):
+                nc.sync.dma_start(plane[first_row + f : P : 32, :].bitcast(I32), rows[f:16:4, :])
 
         def load_rows(raw, matrix):
             nc.sync.dma_start(raw[:], matrix.rearrange("(p j) w -> p j w", j=PACK))
 
         nc.sync.dma_start(offsets[:], offs)
-        load_plane([nc.scalar] * 4, tab_plane, tab_scales)
         load_rows(w1_raw, w1)
+        nc.sync.dma_start(gain_sb[:], gain.rearrange("(p j) o -> p (j o)", j=PACK))
+        nc.sync.dma_start(hsc_sb[:], hsc.rearrange("(p j) o -> p (j o)", j=PACK))
+        load_plane(tab_plane, 0, tab_scales)
         load_words(tab_pool, tab_words)
-        load_plane([nc.gpsimd] * 3 + [nc.scalar], keys_plane, keys_scales)
+        load_rows(query_raw, query)
+        load_plane(keys_plane, KEYS_ROW, keys_scales)
+        load_words(keys_pool, keys_words)
+        load_rows(gout_raw, gout)
+        nc.sync.dma_start(old_sb[:], old)
 
         nc.scalar.activation(warm[:], factors[:, 1:2], ACT.Exp)
 
-        def quantize(name, grouped, width):
-            codes = tile(name + "_codes", [P, width], U32)
+        def quantize(name, grouped, width, tag=None):
+            codes = tile(name + "_codes", [P, width], U32, tag=tag)
             scales = tile(name + "_scales", [P, width], U8)
             nc.vector.quantize_mx(out=codes[:].bitcast(FP8X4), scales=scales[:], in_=grouped)
             return codes, scales
 
+        w1_bf = tile("w1_bf", [P, PACK, P, PACK], BF16)
+        w1_dealt = w1_raw[:].rearrange("p j (m t) -> p m j t", t=PACK)
+        for h, copy in enumerate((nc.vector.tensor_copy, nc.scalar.copy)):
+            places = slice(h * P // 2, (h + 1) * P // 2)
+            copy(w1_bf[:, :, places, :].rearrange("p t m j -> p m j t"), w1_dealt[:, places, :, :])
+
         tab_bytes = tile("tab_bytes", [P, I], U8)
         nc.vector.tensor_copy(tab_bytes[:], tab_plane[:].indirect(offsets[:]))
-        gain_sb = reuse.tile([P, PACK], F32, name="gain_sb", offset=0)
-        hsc_sb = reuse.tile([P, PACK], F32, name="hsc_sb", offset=64)
-        keys_pool = reuse.tile([P, T], U32, name="keys_pool", offset=128)
-        load_words(keys_pool, keys_words)
-        nc.gpsimd.dma_start(gain_sb[:], gain.rearrange("(p j) o -> p (j o)", j=PACK))
-        nc.gpsimd.dma_start(hsc_sb[:], hsc.rearrange("(p j) o -> p (j o)", j=PACK))
-
-        w1_dealt = w1_raw[:].rearrange("p j (m t) -> p m j t", t=PACK)
-        w1_q = []
-        for h, copy in enumerate((nc.vector.tensor_copy, nc.scalar.copy)):
-            grouped = tile("w1_bf%d" % h, [P, 2, P, PACK], BF16)
-            copy(grouped[:].rearrange("p t m j -> p m j t"), w1_dealt[:, :, :, 2 * h : 2 * h + 2])
-            w1_q.append(grouped)
-        query_raw = tile("query_raw", [P, PACK, Q], F32, tag="w1_raw")
-        load_rows(query_raw, query)
-        w1_q[0] = quantize("w1_0", w1_q[0][:].rearrange("p t m j -> p (t m j)"), 2 * P)
-        keys_bytes = tile("keys_bytes", [P, I], U8, tag="w1_bf0")
-        nc.vector.tensor_copy(keys_bytes[:], keys_plane[:].indirect(offsets[:]))
-        w1_q[1] = quantize("w1_1", w1_q[1][:].rearrange("p t m j -> p (t m j)"), 2 * P)
-        gout_raw = tile("gout_raw", [P, PACK, Q], F32, tag="keys_plane")
-        load_rows(gout_raw, gout)
+        w1_codes, w1_scales = quantize("w1", w1_bf[:].rearrange("p t m j -> p (t m j)"), R, tag="tab_plane")
 
         def interleave(name, raw):
             grouped = tile(name + "_bf", [P, Q, PACK], BF16)
@@ -108,77 +106,75 @@ def tile_attend_blrgained_soft_kernel(
             )
             return grouped[:].rearrange("p w j -> p (w j)")
 
-        scale_r = tile("scale_r", [P, PACK], F32)
-        nc.gpsimd.tensor_tensor(scale_r[:], gain_sb[:], hsc_sb[:], ALU.mult)
-        scale_along_slots = scale_r[:].rearrange("p (o t) -> p o t", o=1).to_broadcast([P, CHUNK, PACK])
-
         tab_codes = []
         for h in range(2):
             gathered = tile("tab_codes%d" % h, [P, HALF], U32)
             nc.vector.tensor_copy(gathered[:], tab_pool[:].indirect(offsets[:, 16 * h : 16 * (h + 1)]))
             tab_codes.append(gathered)
-        old_sb = tile("old_sb", [P, T], F32, tag="tab_pool")
-        nc.sync.dma_start(old_sb[:], old)
+        keys_bytes = tile("keys_bytes", [P, I], U8)
+        nc.vector.tensor_copy(keys_bytes[:], keys_plane[:].indirect(offsets[:]))
+        query_codes, query_scales = quantize("query", interleave("query", query_raw), Q)
+
+        scale_r = tile("scale_r", [P, PACK], F32)
+        nc.vector.tensor_tensor(scale_r[:], gain_sb[:], hsc_sb[:], ALU.mult)
+        scale_along_slots = scale_r[:].rearrange("p (o t) -> p o t", o=1).to_broadcast([P, CHUNK, PACK])
 
         ht = []
         for c in range(I // CHUNK):
             zh = psum.tile([P, PACK, CHUNK], F32, name="zh%d" % c)
             first = (c * CHUNK) % HALF
             for t in range(PACK):
-                codes, scales = w1_q[t // 2]
-                cols = slice((t % 2) * P, (t % 2 + 1) * P)
+                cols = slice(t * P, (t + 1) * P)
                 nc.tensor.matmul_mx(
                     out=zh[:, t, :],
-                    lhsT=codes[:, cols].bitcast(FP8X4),
-                    lhsT_scale=scales[:, cols],
+                    lhsT=w1_codes[:, cols].bitcast(FP8X4),
+                    lhsT_scale=w1_scales[:, cols],
                     rhs=tab_codes[c * CHUNK // HALF][:, first : first + CHUNK].bitcast(FP8X4),
                     rhs_scale=tab_bytes[:, c * CHUNK : (c + 1) * CHUNK],
                     start=True,
                     stop=True,
                 )
-            ht_c = tile("ht%d" % c, [P, CHUNK, PACK], F32)
+            ht_c = tile("ht%d" % c, [P, CHUNK, PACK], F32, tag="query_raw" if c == 0 else None)
             nc.scalar.activation(ht_c[:], zh[:].rearrange("p t n -> p n t"), ACT.Tanh)
             ht.append(ht_c)
 
-        query_bf = interleave("query", query_raw)
         gout_bf = interleave("gout", gout_raw)
 
         c0 = psum.tile([P, I], F32, name="c0")
         hs1_bf = {}
         hs1_q = {}
 
-        def scale_chunk(c):
-            hs1_bf[c] = tile("hs1_bf%d" % c, [P, CHUNK, PACK], BF16)
+        def scale_chunk(c, tag=None):
+            hs1_bf[c] = tile("hs1_bf%d" % c, [P, CHUNK, PACK], BF16, tag=tag)
             nc.vector.tensor_tensor(hs1_bf[c][:], ht[c][:], scale_along_slots, ALU.mult)
 
         def quantize_chunk(c):
             hs1_q[c] = quantize("hs1_%d" % c, hs1_bf[c][:].rearrange("p n t -> p (n t)"), CHUNK)
 
-        scale_chunk(0)
+        scale_chunk(0, tag="keys_plane")
         scale_chunk(1)
         quantize_chunk(0)
         keys_codes = tile("keys_codes", [P, I], U32)
         nc.vector.tensor_copy(keys_codes[:], keys_pool[:].indirect(offsets[:]))
-        query_codes, query_scales = quantize("query", query_bf, Q)
         a = psum.tile([P, I], F32, name="a")
         nc.tensor.matmul_mx(
             out=a[:],
             lhsT=query_codes[:].bitcast(FP8X4),
             lhsT_scale=query_scales[:],
             rhs=keys_codes[:].bitcast(FP8X4),
-            rhs_scale=keys_bytes[:],
+            rhs_scale=keys_bytes[KEYS_ROW:P, :],
             start=True,
             stop=True,
         )
         quantize_chunk(1)
-        scale_chunk(2)
+        scale_chunk(2, tag="keys_pool")
         neg_max = tile("neg_max", [P, 1], F32)
         nc.vector.tensor_reduce(neg_max[:], a[:], AXIS.X, ALU.max, negate=True)
         p = tile("p", [P, I], F32)
         z = tile("z", [P, 1], F32)
         nc.scalar.activation(p[:], a[:], ACT.Exp, bias=neg_max[:], accum_out=z[:])
         gout_codes, gout_scales = quantize("gout", gout_bf, Q)
-        scale_chunk(3)
+        scale_chunk(3, tag="keys_codes")
         quantize_chunk(2)
         quantize_chunk(3)
         for c in range(I // CHUNK):

@@ -31,6 +31,7 @@ def tile_attend_blrgained_soft_kernel(
 
     with ExitStack() as ctx:
         sb = ctx.enter_context(tc.tile_pool(name="sb", bufs=1))
+        reuse = ctx.enter_context(tc.tile_pool(name="reuse", bufs=1))
         psum = ctx.enter_context(tc.psum_pool(name="psum", bufs=1))
 
         def tile(name, shape, dtype, tag=None):
@@ -38,7 +39,7 @@ def tile_attend_blrgained_soft_kernel(
 
         offsets = tile("offsets", [P, I // 16], U16)
         tab_pool = tile("tab_pool", [P, T], U32)
-        keys_pool = tile("keys_pool", [P, T], U32)
+        keys_pool = reuse.tile([P, T], U32, name="keys_pool", offset=0, align_bytes=64)
         tab_plane = tile("tab_plane", [P, T], U8)
         keys_plane = tile("keys_plane", [P, T], U8)
         w1_raw = tile("w1_raw", [P, PACK, R], F32)
@@ -82,8 +83,8 @@ def tile_attend_blrgained_soft_kernel(
 
         nc.scalar.activation(warm[:], factors[:, 1:2], ACT.Exp)
 
-        def quantize(name, grouped, width, tag=None):
-            codes = tile(name + "_codes", [P, width], U32, tag=tag)
+        def quantize(name, grouped, codes):
+            width = codes.shape[1]
             scales = tile(name + "_scales", [P, width], U8)
             nc.vector.quantize_mx(out=codes[:].bitcast(FP8X4), scales=scales[:], in_=grouped)
             return codes, scales
@@ -96,7 +97,7 @@ def tile_attend_blrgained_soft_kernel(
 
         tab_bytes = tile("tab_bytes", [P, I], U8)
         nc.vector.tensor_copy(tab_bytes[:], tab_plane[:].indirect(offsets[:]))
-        w1_codes, w1_scales = quantize("w1", w1_bf[:].rearrange("p t m j -> p (t m j)"), R, tag="tab_plane")
+        w1_codes, w1_scales = quantize("w1", w1_bf[:].rearrange("p t m j -> p (t m j)"), tile("w1_codes", [P, R], U32, tag="tab_plane"))
 
         def interleave(name, raw):
             grouped = tile(name + "_bf", [P, Q, PACK], BF16)
@@ -113,13 +114,13 @@ def tile_attend_blrgained_soft_kernel(
             tab_codes.append(gathered)
         keys_bytes = tile("keys_bytes", [P, I], U8)
         nc.vector.tensor_copy(keys_bytes[:], keys_plane[:].indirect(offsets[:]))
-        query_codes, query_scales = quantize("query", interleave("query", query_raw), Q)
+        query_codes, query_scales = quantize("query", interleave("query", query_raw), tile("query_codes", [P, Q], U32))
 
         scale_r = tile("scale_r", [P, PACK], F32)
         nc.vector.tensor_tensor(scale_r[:], gain_sb[:], hsc_sb[:], ALU.mult)
         scale_along_slots = scale_r[:].rearrange("p (o t) -> p o t", o=1).to_broadcast([P, CHUNK, PACK])
 
-        ht = []
+        ht = tile("ht", [P, I // CHUNK, CHUNK, PACK], F32, tag="query_raw")
         for c in range(I // CHUNK):
             zh = psum.tile([P, PACK, CHUNK], F32, name="zh%d" % c)
             first = (c * CHUNK) % HALF
@@ -134,26 +135,16 @@ def tile_attend_blrgained_soft_kernel(
                     start=True,
                     stop=True,
                 )
-            ht_c = tile("ht%d" % c, [P, CHUNK, PACK], F32, tag="query_raw" if c == 0 else None)
-            nc.scalar.activation(ht_c[:], zh[:].rearrange("p t n -> p n t"), ACT.Tanh)
-            ht.append(ht_c)
+            nc.scalar.activation(ht[:, c], zh[:].rearrange("p t n -> p n t"), ACT.Tanh)
 
         gout_bf = interleave("gout", gout_raw)
 
-        c0 = psum.tile([P, I], F32, name="c0")
-        hs1_bf = {}
-        hs1_q = {}
+        def scale_chunk(c, hs1_bf):
+            nc.vector.tensor_tensor(hs1_bf, ht[:, c], scale_along_slots, ALU.mult)
 
-        def scale_chunk(c, tag=None):
-            hs1_bf[c] = tile("hs1_bf%d" % c, [P, CHUNK, PACK], BF16, tag=tag)
-            nc.vector.tensor_tensor(hs1_bf[c][:], ht[c][:], scale_along_slots, ALU.mult)
-
-        def quantize_chunk(c):
-            hs1_q[c] = quantize("hs1_%d" % c, hs1_bf[c][:].rearrange("p n t -> p (n t)"), CHUNK)
-
-        scale_chunk(0, tag="keys_plane")
-        scale_chunk(1)
-        quantize_chunk(0)
+        hs1_first = tile("hs1_first", [P, 2, CHUNK, PACK], BF16, tag="keys_plane")
+        scale_chunk(0, hs1_first[:, 0])
+        scale_chunk(1, hs1_first[:, 1])
         keys_codes = tile("keys_codes", [P, I], U32)
         nc.vector.tensor_copy(keys_codes[:], keys_pool[:].indirect(offsets[:]))
         a = psum.tile([P, I], F32, name="a")
@@ -166,21 +157,28 @@ def tile_attend_blrgained_soft_kernel(
             start=True,
             stop=True,
         )
-        quantize_chunk(1)
-        scale_chunk(2, tag="keys_pool")
+        hs1_q = [quantize("hs1_first", hs1_first[:].rearrange("p c n t -> p (c n t)"), tile("hs1_first_codes", [P, 2 * CHUNK], U32))]
+        hs1_third = reuse.tile([P, CHUNK, PACK], BF16, name="hs1_third", offset=0, align_bytes=64)
+        scale_chunk(2, hs1_third[:])
         neg_max = tile("neg_max", [P, 1], F32)
         nc.vector.tensor_reduce(neg_max[:], a[:], AXIS.X, ALU.max, negate=True)
         p = tile("p", [P, I], F32)
         z = tile("z", [P, 1], F32)
         nc.scalar.activation(p[:], a[:], ACT.Exp, bias=neg_max[:], accum_out=z[:])
-        gout_codes, gout_scales = quantize("gout", gout_bf, Q)
-        scale_chunk(3, tag="keys_codes")
-        quantize_chunk(2)
-        quantize_chunk(3)
-        for c in range(I // CHUNK):
-            codes, scales = hs1_q[c]
+        hs1_last = tile("hs1_last", [P, CHUNK, PACK], BF16, tag="keys_codes")
+        scale_chunk(3, hs1_last[:])
+        gout_codes, gout_scales = quantize(
+            "gout", gout_bf, reuse.tile([P, Q], U32, name="gout_codes", offset=1024, align_bytes=64)
+        )
+        hs1_q.append(quantize("hs1_third", hs1_third[:].rearrange("p n t -> p (n t)"), tile("hs1_third_codes", [P, CHUNK], U32)))
+        hs1_q.append(quantize("hs1_last", hs1_last[:].rearrange("p n t -> p (n t)"), tile("hs1_last_codes", [P, CHUNK], U32)))
+
+        c0 = psum.tile([P, I], F32, name="c0")
+        first = 0
+        for codes, scales in hs1_q:
+            width = codes.shape[1]
             nc.tensor.matmul_mx(
-                out=c0[:, c * CHUNK : (c + 1) * CHUNK],
+                out=c0[:, first : first + width],
                 lhsT=gout_codes[:].bitcast(FP8X4),
                 lhsT_scale=gout_scales[:],
                 rhs=codes[:].bitcast(FP8X4),
@@ -188,6 +186,7 @@ def tile_attend_blrgained_soft_kernel(
                 start=True,
                 stop=True,
             )
+            first += width
 
         over_z = tile("over_z", [P, 1], F32)
         nc.vector.reciprocal(over_z[:], z[:])

@@ -21,6 +21,7 @@ PACK = 4
 CHUNK = 128
 HALF = I // 2
 KEYS_ROW = 4
+W1_ON_VECTOR = 48
 STORE_WIDTHS = (256, 512, 512, 512, 256)
 
 
@@ -50,13 +51,12 @@ def tile_attend_blrgained_soft_kernel(
         old_sb = tile("old_sb", [P, T], F32)
         window = tile("window", [P, T], F32)
         factors = tile("factors", [P, 2], F32)
-        warm = tile("warm", [P, 1], F32)
 
         nc.vector.memset(tab_plane[:].bitcast(I32), 0)
         nc.vector.memset(keys_plane[:].bitcast(I32), 0)
         nc.vector.memset(factors[:, 0:1], 512.0)
         nc.vector.memset(factors[:, 1:2], -1.0)
-        nc.gpsimd.memset(window[:], 0.0)
+        nc.vector.memset(window[:], 0.0)
 
         def load_words(pool_tile, words):
             nc.sync.dma_start(pool_tile[:].bitcast(I32), words[0].rearrange("p n t -> p (n t)").bitcast(I32))
@@ -81,8 +81,6 @@ def tile_attend_blrgained_soft_kernel(
         load_rows(gout_raw, gout)
         nc.sync.dma_start(old_sb[:], old)
 
-        nc.scalar.activation(warm[:], factors[:, 1:2], ACT.Exp)
-
         def quantize(name, grouped, codes):
             width = codes.shape[1]
             scales = tile(name + "_scales", [P, width], U8)
@@ -91,9 +89,9 @@ def tile_attend_blrgained_soft_kernel(
 
         w1_bf = tile("w1_bf", [P, PACK, P, PACK], BF16)
         w1_dealt = w1_raw[:].rearrange("p j (m t) -> p m j t", t=PACK)
-        for h, copy in enumerate((nc.vector.tensor_copy, nc.scalar.copy)):
-            places = slice(h * P // 2, (h + 1) * P // 2)
-            copy(w1_bf[:, :, places, :].rearrange("p t m j -> p m j t"), w1_dealt[:, places, :, :])
+        w1_walk = w1_bf[:].rearrange("p t m j -> p m j t")
+        nc.vector.tensor_copy(w1_walk[:, :W1_ON_VECTOR], w1_dealt[:, :W1_ON_VECTOR])
+        nc.scalar.activation(w1_walk[:, W1_ON_VECTOR:], w1_dealt[:, W1_ON_VECTOR:], ACT.Copy)
 
         tab_bytes = tile("tab_bytes", [P, I], U8)
         nc.vector.tensor_copy(tab_bytes[:], tab_plane[:].indirect(offsets[:]))
@@ -107,11 +105,11 @@ def tile_attend_blrgained_soft_kernel(
             )
             return grouped[:].rearrange("p w j -> p (w j)")
 
-        tab_codes = []
+        tab_codes = tile("tab_codes", [P, I], U32, tag="w1_bf")
         for h in range(2):
-            gathered = tile("tab_codes%d" % h, [P, HALF], U32)
-            nc.vector.tensor_copy(gathered[:], tab_pool[:].indirect(offsets[:, 16 * h : 16 * (h + 1)]))
-            tab_codes.append(gathered)
+            nc.vector.tensor_copy(
+                tab_codes[:, h * HALF : (h + 1) * HALF], tab_pool[:].indirect(offsets[:, 16 * h : 16 * (h + 1)])
+            )
         keys_bytes = tile("keys_bytes", [P, I], U8)
         nc.vector.tensor_copy(keys_bytes[:], keys_plane[:].indirect(offsets[:]))
         query_codes, query_scales = quantize("query", interleave("query", query_raw), tile("query_codes", [P, Q], U32))
@@ -123,14 +121,13 @@ def tile_attend_blrgained_soft_kernel(
         ht = tile("ht", [P, I // CHUNK, CHUNK, PACK], F32, tag="query_raw")
         for c in range(I // CHUNK):
             zh = psum.tile([P, PACK, CHUNK], F32, name="zh%d" % c)
-            first = (c * CHUNK) % HALF
             for t in range(PACK):
                 cols = slice(t * P, (t + 1) * P)
                 nc.tensor.matmul_mx(
                     out=zh[:, t, :],
                     lhsT=w1_codes[:, cols].bitcast(FP8X4),
                     lhsT_scale=w1_scales[:, cols],
-                    rhs=tab_codes[c * CHUNK // HALF][:, first : first + CHUNK].bitcast(FP8X4),
+                    rhs=tab_codes[:, c * CHUNK : (c + 1) * CHUNK].bitcast(FP8X4),
                     rhs_scale=tab_bytes[:, c * CHUNK : (c + 1) * CHUNK],
                     start=True,
                     stop=True,

@@ -18,11 +18,17 @@ AXIS = mybir.AxisListType
 
 P = 128
 PACK = 4
+QUADRANT = 32
+BLOCKS = 16
+GROUP = 16
 CHUNK = 128
+CHUNKS = I // CHUNK
 HALF = I // 2
+GRAD_SCALE = 512.0
 KEYS_ROW = 4
 W1_ON_VECTOR = 48
 STORE_WIDTHS = (256, 512, 512, 512, 256)
+ALIGN = 64
 
 
 def tile_attend_blrgained_soft_kernel(
@@ -32,15 +38,18 @@ def tile_attend_blrgained_soft_kernel(
 
     with ExitStack() as ctx:
         sb = ctx.enter_context(tc.tile_pool(name="sb", bufs=1))
-        reuse = ctx.enter_context(tc.tile_pool(name="reuse", bufs=1))
+        keys_bytes_pool = ctx.enter_context(tc.tile_pool(name="reuse", bufs=1))
         psum = ctx.enter_context(tc.psum_pool(name="psum", bufs=1))
 
         def tile(name, shape, dtype, tag=None):
-            return sb.tile(shape, dtype, name=name, tag=tag or name, align_bytes=64)
+            return sb.tile(shape, dtype, name=name, tag=tag or name, align_bytes=ALIGN)
 
-        offsets = tile("offsets", [P, I // 16], U16)
+        def on_keys_pool(name, shape, dtype, offset):
+            return keys_bytes_pool.tile(shape, dtype, name=name, offset=offset, align_bytes=ALIGN)
+
+        offsets = tile("offsets", [P, I // GROUP], U16)
         tab_pool = tile("tab_pool", [P, T], U32)
-        keys_pool = reuse.tile([P, T], U32, name="keys_pool", offset=0, align_bytes=64)
+        keys_pool = on_keys_pool("keys_pool", [P, T], U32, 0)
         tab_plane = tile("tab_plane", [P, T], U8)
         keys_plane = tile("keys_plane", [P, T], U8)
         w1_raw = tile("w1_raw", [P, PACK, R], F32)
@@ -54,7 +63,7 @@ def tile_attend_blrgained_soft_kernel(
 
         nc.vector.memset(tab_plane[:].bitcast(I32), 0)
         nc.vector.memset(keys_plane[:].bitcast(I32), 0)
-        nc.vector.memset(factors[:, 0:1], 512.0)
+        nc.vector.memset(factors[:, 0:1], GRAD_SCALE)
         nc.vector.memset(factors[:, 1:2], -1.0)
         nc.vector.memset(window[:], 0.0)
 
@@ -63,8 +72,8 @@ def tile_attend_blrgained_soft_kernel(
 
         def load_plane(plane, first_row, scales):
             rows = scales[0].bitcast(I32)
-            for f in range(4):
-                nc.sync.dma_start(plane[first_row + f : P : 32, :].bitcast(I32), rows[f:16:4, :])
+            for f in range(PACK):
+                nc.sync.dma_start(plane[first_row + f : P : QUADRANT, :].bitcast(I32), rows[f:BLOCKS:PACK, :])
 
         def load_rows(raw, matrix):
             nc.sync.dma_start(raw[:], matrix.rearrange("(p j) w -> p j w", j=PACK))
@@ -87,6 +96,25 @@ def tile_attend_blrgained_soft_kernel(
             nc.vector.quantize_mx(out=codes[:].bitcast(FP8X4), scales=scales[:], in_=grouped)
             return codes, scales
 
+        def product(result, stationary, stationary_scales, moving, moving_scales):
+            nc.tensor.matmul_mx(
+                out=result,
+                lhsT=stationary.bitcast(FP8X4),
+                lhsT_scale=stationary_scales,
+                rhs=moving.bitcast(FP8X4),
+                rhs_scale=moving_scales,
+                start=True,
+                stop=True,
+            )
+
+        def interleave(name, raw):
+            grouped = tile(name + "_bf", [P, raw.shape[2], PACK], BF16)
+            nc.scalar.copy(
+                grouped[:].rearrange("p (c i) j -> p c j i", i=4),
+                raw[:].rearrange("p j (c i) -> p c j i", i=4),
+            )
+            return grouped[:].rearrange("p w j -> p (w j)")
+
         w1_bf = tile("w1_bf", [P, PACK, P, PACK], BF16)
         w1_dealt = w1_raw[:].rearrange("p j (m t) -> p m j t", t=PACK)
         w1_walk = w1_bf[:].rearrange("p t m j -> p m j t")
@@ -95,20 +123,15 @@ def tile_attend_blrgained_soft_kernel(
 
         tab_bytes = tile("tab_bytes", [P, I], U8)
         nc.vector.tensor_copy(tab_bytes[:], tab_plane[:].indirect(offsets[:]))
-        w1_codes, w1_scales = quantize("w1", w1_bf[:].rearrange("p t m j -> p (t m j)"), tile("w1_codes", [P, R], U32, tag="tab_plane"))
-
-        def interleave(name, raw):
-            grouped = tile(name + "_bf", [P, Q, PACK], BF16)
-            nc.scalar.copy(
-                grouped[:].rearrange("p (c i) j -> p c j i", i=4),
-                raw[:].rearrange("p j (c i) -> p c j i", i=4),
-            )
-            return grouped[:].rearrange("p w j -> p (w j)")
+        w1_codes, w1_scales = quantize(
+            "w1", w1_bf[:].rearrange("p t m j -> p (t m j)"), tile("w1_codes", [P, R], U32, tag="tab_plane")
+        )
 
         tab_codes = tile("tab_codes", [P, I], U32, tag="w1_bf")
-        for h in range(2):
+        for first in range(0, I, HALF):
             nc.vector.tensor_copy(
-                tab_codes[:, h * HALF : (h + 1) * HALF], tab_pool[:].indirect(offsets[:, 16 * h : 16 * (h + 1)])
+                tab_codes[:, first : first + HALF],
+                tab_pool[:].indirect(offsets[:, first // GROUP : (first + HALF) // GROUP]),
             )
         keys_bytes = tile("keys_bytes", [P, I], U8)
         nc.vector.tensor_copy(keys_bytes[:], keys_plane[:].indirect(offsets[:]))
@@ -118,71 +141,64 @@ def tile_attend_blrgained_soft_kernel(
         nc.vector.tensor_tensor(scale_r[:], gain_sb[:], hsc_sb[:], ALU.mult)
         scale_along_slots = scale_r[:].rearrange("p (o t) -> p o t", o=1).to_broadcast([P, CHUNK, PACK])
 
-        ht = tile("ht", [P, I // CHUNK, CHUNK, PACK], F32, tag="query_raw")
-        for c in range(I // CHUNK):
+        ht = tile("ht", [P, CHUNKS, CHUNK * PACK], F32, tag="query_raw")
+        last = CHUNKS - 1
+        for c in range(CHUNKS):
             zh = psum.tile([P, PACK, CHUNK], F32, name="zh%d" % c)
+            slots = slice(c * CHUNK, (c + 1) * CHUNK)
             for t in range(PACK):
                 cols = slice(t * P, (t + 1) * P)
-                nc.tensor.matmul_mx(
-                    out=zh[:, t, :],
-                    lhsT=w1_codes[:, cols].bitcast(FP8X4),
-                    lhsT_scale=w1_scales[:, cols],
-                    rhs=tab_codes[:, c * CHUNK : (c + 1) * CHUNK].bitcast(FP8X4),
-                    rhs_scale=tab_bytes[:, c * CHUNK : (c + 1) * CHUNK],
-                    start=True,
-                    stop=True,
+                product(zh[:, t, :], w1_codes[:, cols], w1_scales[:, cols], tab_codes[:, slots], tab_bytes[:, slots])
+            if c < last:
+                nc.scalar.activation(
+                    ht[:, c].rearrange("p (n t) -> p n t", t=PACK), zh[:].rearrange("p t n -> p n t"), ACT.Tanh
                 )
-            nc.scalar.activation(ht[:, c], zh[:].rearrange("p t n -> p n t"), ACT.Tanh)
+            else:
+                nc.scalar.activation(ht[:, c], zh[:].rearrange("p t n -> p (t n)"), ACT.Tanh)
 
         gout_bf = interleave("gout", gout_raw)
 
+        hs1_by_place = tile("hs1_by_place", [P, PACK, CHUNK], BF16)
+        for t in range(PACK):
+            nc.scalar.activation(
+                hs1_by_place[:, t, :], ht[:, last, t * CHUNK : (t + 1) * CHUNK], ACT.Copy, scale=scale_r[:, t : t + 1]
+            )
+        hs1_last = interleave("hs1_last", hs1_by_place)
+
         def scale_chunk(c, hs1_bf):
-            nc.vector.tensor_tensor(hs1_bf, ht[:, c], scale_along_slots, ALU.mult)
+            nc.vector.tensor_tensor(hs1_bf, ht[:, c].rearrange("p (n t) -> p n t", t=PACK), scale_along_slots, ALU.mult)
 
         hs1_first = tile("hs1_first", [P, 2, CHUNK, PACK], BF16, tag="keys_plane")
         scale_chunk(0, hs1_first[:, 0])
         scale_chunk(1, hs1_first[:, 1])
+
         keys_codes = tile("keys_codes", [P, I], U32)
         nc.vector.tensor_copy(keys_codes[:], keys_pool[:].indirect(offsets[:]))
         a = psum.tile([P, I], F32, name="a")
-        nc.tensor.matmul_mx(
-            out=a[:],
-            lhsT=query_codes[:].bitcast(FP8X4),
-            lhsT_scale=query_scales[:],
-            rhs=keys_codes[:].bitcast(FP8X4),
-            rhs_scale=keys_bytes[KEYS_ROW:P, :],
-            start=True,
-            stop=True,
-        )
-        hs1_q = [quantize("hs1_first", hs1_first[:].rearrange("p c n t -> p (c n t)"), tile("hs1_first_codes", [P, 2 * CHUNK], U32))]
-        hs1_third = reuse.tile([P, CHUNK, PACK], BF16, name="hs1_third", offset=0, align_bytes=64)
+        product(a[:], query_codes[:], query_scales[:], keys_codes[:], keys_bytes[KEYS_ROW:P, :])
+
+        hs1_third = on_keys_pool("hs1_third", [P, CHUNK, PACK], BF16, 0)
+        gout_words = on_keys_pool("gout_codes", [P, Q], U32, 1024)
+        first_words = on_keys_pool("hs1_first_codes", [P, 2 * CHUNK], U32, 2048)
+
         scale_chunk(2, hs1_third[:])
+        hs1_q = [quantize("hs1_first", hs1_first[:].rearrange("p c n t -> p (c n t)"), first_words)]
         neg_max = tile("neg_max", [P, 1], F32)
         nc.vector.tensor_reduce(neg_max[:], a[:], AXIS.X, ALU.max, negate=True)
         p = tile("p", [P, I], F32)
         z = tile("z", [P, 1], F32)
         nc.scalar.activation(p[:], a[:], ACT.Exp, bias=neg_max[:], accum_out=z[:])
-        hs1_last = tile("hs1_last", [P, CHUNK, PACK], BF16, tag="keys_codes")
-        scale_chunk(3, hs1_last[:])
-        gout_codes, gout_scales = quantize(
-            "gout", gout_bf, reuse.tile([P, Q], U32, name="gout_codes", offset=1024, align_bytes=64)
+        gout_codes, gout_scales = quantize("gout", gout_bf, gout_words)
+        hs1_q.append(
+            quantize("hs1_third", hs1_third[:].rearrange("p n t -> p (n t)"), tile("hs1_third_codes", [P, CHUNK], U32))
         )
-        hs1_q.append(quantize("hs1_third", hs1_third[:].rearrange("p n t -> p (n t)"), tile("hs1_third_codes", [P, CHUNK], U32)))
-        hs1_q.append(quantize("hs1_last", hs1_last[:].rearrange("p n t -> p (n t)"), tile("hs1_last_codes", [P, CHUNK], U32)))
+        hs1_q.append(quantize("hs1_last", hs1_last, tile("hs1_last_codes", [P, CHUNK], U32, tag="keys_codes")))
 
         c0 = psum.tile([P, I], F32, name="c0")
         first = 0
         for codes, scales in hs1_q:
             width = codes.shape[1]
-            nc.tensor.matmul_mx(
-                out=c0[:, first : first + width],
-                lhsT=gout_codes[:].bitcast(FP8X4),
-                lhsT_scale=gout_scales[:],
-                rhs=codes[:].bitcast(FP8X4),
-                rhs_scale=scales[:],
-                start=True,
-                stop=True,
-            )
+            product(c0[:, first : first + width], gout_codes[:], gout_scales[:], codes[:], scales[:])
             first += width
 
         over_z = tile("over_z", [P, 1], F32)

from contextlib import ExitStack

import concourse.mybir as mybir

D, K, R, T, I, Q = 512, 512, 512, 2048, 512, 128
FLOPS = 2 * (D * Q * I + K * R * I + R * Q * I)

F32 = mybir.dt.float32
BF16 = mybir.dt.bfloat16
I32 = mybir.dt.int32
U32 = mybir.dt.uint32
U16 = mybir.dt.uint16
U8 = mybir.dt.uint8
FP8X4 = mybir.dt.float8_e4m3fn_x4
ALU = mybir.AluOpType
ACT = mybir.ActivationFunctionType
AXIS = mybir.AxisListType

P = 128
PACK = 4
QUADRANT = 32
BLOCKS = 16
GROUP = 16
CHUNK = 128
CHUNKS = I // CHUNK
HALF = I // 2
GRAD_SCALE = 512.0
KEYS_ROW = 4
W1_ON_VECTOR = 48
STORE_WIDTHS = (256, 512, 512, 512, 256)
ALIGN = 64


def tile_attend_blrgained_soft_kernel(
    tc, query, keys_words, keys_scales, tab_words, tab_scales, w1, gain, gout, hsc, old, offs, out
):
    nc = tc.nc

    with ExitStack() as ctx:
        sb = ctx.enter_context(tc.tile_pool(name="sb", bufs=1))
        keys_bytes_pool = ctx.enter_context(tc.tile_pool(name="reuse", bufs=1))
        psum = ctx.enter_context(tc.psum_pool(name="psum", bufs=1))

        def tile(name, shape, dtype, tag=None):
            return sb.tile(shape, dtype, name=name, tag=tag or name, align_bytes=ALIGN)

        def on_keys_pool(name, shape, dtype, offset):
            return keys_bytes_pool.tile(shape, dtype, name=name, offset=offset, align_bytes=ALIGN)

        offsets = tile("offsets", [P, I // GROUP], U16)
        tab_pool = tile("tab_pool", [P, T], U32)
        keys_pool = on_keys_pool("keys_pool", [P, T], U32, 0)
        tab_plane = tile("tab_plane", [P, T], U8)
        keys_plane = tile("keys_plane", [P, T], U8)
        w1_raw = tile("w1_raw", [P, PACK, R], F32)
        query_raw = tile("query_raw", [P, PACK, Q], F32)
        gout_raw = tile("gout_raw", [P, PACK, Q], F32)
        gain_sb = tile("gain_sb", [P, PACK], F32)
        hsc_sb = tile("hsc_sb", [P, PACK], F32)
        old_sb = tile("old_sb", [P, T], F32)
        window = tile("window", [P, T], F32)
        factors = tile("factors", [P, 2], F32)

        nc.vector.memset(tab_plane[:].bitcast(I32), 0)
        nc.vector.memset(keys_plane[:].bitcast(I32), 0)
        nc.vector.memset(factors[:, 0:1], GRAD_SCALE)
        nc.vector.memset(factors[:, 1:2], -1.0)
        nc.vector.memset(window[:], 0.0)

        def load_words(pool_tile, words):
            nc.sync.dma_start(pool_tile[:].bitcast(I32), words[0].rearrange("p n t -> p (n t)").bitcast(I32))

        def load_plane(plane, first_row, scales):
            rows = scales[0].bitcast(I32)
            for f in range(PACK):
                nc.sync.dma_start(plane[first_row + f : P : QUADRANT, :].bitcast(I32), rows[f:BLOCKS:PACK, :])

        def load_rows(raw, matrix):
            nc.sync.dma_start(raw[:], matrix.rearrange("(p j) w -> p j w", j=PACK))

        nc.sync.dma_start(offsets[:], offs)
        load_rows(w1_raw, w1)
        nc.sync.dma_start(gain_sb[:], gain.rearrange("(p j) o -> p (j o)", j=PACK))
        nc.sync.dma_start(hsc_sb[:], hsc.rearrange("(p j) o -> p (j o)", j=PACK))
        load_plane(tab_plane, 0, tab_scales)
        load_words(tab_pool, tab_words)
        load_rows(query_raw, query)
        load_plane(keys_plane, KEYS_ROW, keys_scales)
        load_words(keys_pool, keys_words)
        load_rows(gout_raw, gout)
        nc.sync.dma_start(old_sb[:], old)

        def quantize(name, grouped, codes):
            width = codes.shape[1]
            scales = tile(name + "_scales", [P, width], U8)
            nc.vector.quantize_mx(out=codes[:].bitcast(FP8X4), scales=scales[:], in_=grouped)
            return codes, scales

        def product(result, stationary, stationary_scales, moving, moving_scales):
            nc.tensor.matmul_mx(
                out=result,
                lhsT=stationary.bitcast(FP8X4),
                lhsT_scale=stationary_scales,
                rhs=moving.bitcast(FP8X4),
                rhs_scale=moving_scales,
                start=True,
                stop=True,
            )

        def interleave(name, raw):
            grouped = tile(name + "_bf", [P, raw.shape[2], PACK], BF16)
            nc.scalar.copy(
                grouped[:].rearrange("p (c i) j -> p c j i", i=4),
                raw[:].rearrange("p j (c i) -> p c j i", i=4),
            )
            return grouped[:].rearrange("p w j -> p (w j)")

        w1_bf = tile("w1_bf", [P, PACK, P, PACK], BF16)
        w1_dealt = w1_raw[:].rearrange("p j (m t) -> p m j t", t=PACK)
        w1_walk = w1_bf[:].rearrange("p t m j -> p m j t")
        nc.vector.tensor_copy(w1_walk[:, :W1_ON_VECTOR], w1_dealt[:, :W1_ON_VECTOR])
        nc.scalar.activation(w1_walk[:, W1_ON_VECTOR:], w1_dealt[:, W1_ON_VECTOR:], ACT.Copy)

        tab_bytes = tile("tab_bytes", [P, I], U8)
        nc.vector.tensor_copy(tab_bytes[:], tab_plane[:].indirect(offsets[:]))
        w1_codes, w1_scales = quantize(
            "w1", w1_bf[:].rearrange("p t m j -> p (t m j)"), tile("w1_codes", [P, R], U32, tag="tab_plane")
        )

        tab_codes = tile("tab_codes", [P, I], U32, tag="w1_bf")
        for first in range(0, I, HALF):
            nc.vector.tensor_copy(
                tab_codes[:, first : first + HALF],
                tab_pool[:].indirect(offsets[:, first // GROUP : (first + HALF) // GROUP]),
            )
        keys_bytes = tile("keys_bytes", [P, I], U8)
        nc.vector.tensor_copy(keys_bytes[:], keys_plane[:].indirect(offsets[:]))
        query_codes, query_scales = quantize("query", interleave("query", query_raw), tile("query_codes", [P, Q], U32))

        scale_r = tile("scale_r", [P, PACK], F32)
        nc.vector.tensor_tensor(scale_r[:], gain_sb[:], hsc_sb[:], ALU.mult)
        scale_along_slots = scale_r[:].rearrange("p (o t) -> p o t", o=1).to_broadcast([P, CHUNK, PACK])

        ht = tile("ht", [P, CHUNKS, CHUNK * PACK], F32, tag="query_raw")
        last = CHUNKS - 1
        for c in range(CHUNKS):
            zh = psum.tile([P, PACK, CHUNK], F32, name="zh%d" % c)
            slots = slice(c * CHUNK, (c + 1) * CHUNK)
            for t in range(PACK):
                cols = slice(t * P, (t + 1) * P)
                product(zh[:, t, :], w1_codes[:, cols], w1_scales[:, cols], tab_codes[:, slots], tab_bytes[:, slots])
            if c < last:
                nc.scalar.activation(
                    ht[:, c].rearrange("p (n t) -> p n t", t=PACK), zh[:].rearrange("p t n -> p n t"), ACT.Tanh
                )
            else:
                nc.scalar.activation(ht[:, c], zh[:].rearrange("p t n -> p (t n)"), ACT.Tanh)

        gout_bf = interleave("gout", gout_raw)

        hs1_by_place = tile("hs1_by_place", [P, PACK, CHUNK], BF16)
        for t in range(PACK):
            nc.scalar.activation(
                hs1_by_place[:, t, :], ht[:, last, t * CHUNK : (t + 1) * CHUNK], ACT.Copy, scale=scale_r[:, t : t + 1]
            )
        hs1_last = interleave("hs1_last", hs1_by_place)

        def scale_chunk(c, hs1_bf):
            nc.vector.tensor_tensor(hs1_bf, ht[:, c].rearrange("p (n t) -> p n t", t=PACK), scale_along_slots, ALU.mult)

        hs1_first = tile("hs1_first", [P, 2, CHUNK, PACK], BF16, tag="keys_plane")
        scale_chunk(0, hs1_first[:, 0])
        scale_chunk(1, hs1_first[:, 1])

        keys_codes = tile("keys_codes", [P, I], U32)
        nc.vector.tensor_copy(keys_codes[:], keys_pool[:].indirect(offsets[:]))
        a = psum.tile([P, I], F32, name="a")
        product(a[:], query_codes[:], query_scales[:], keys_codes[:], keys_bytes[KEYS_ROW:P, :])

        hs1_third = on_keys_pool("hs1_third", [P, CHUNK, PACK], BF16, 0)
        gout_words = on_keys_pool("gout_codes", [P, Q], U32, 1024)
        first_words = on_keys_pool("hs1_first_codes", [P, 2 * CHUNK], U32, 2048)

        scale_chunk(2, hs1_third[:])
        hs1_q = [quantize("hs1_first", hs1_first[:].rearrange("p c n t -> p (c n t)"), first_words)]
        neg_max = tile("neg_max", [P, 1], F32)
        nc.vector.tensor_reduce(neg_max[:], a[:], AXIS.X, ALU.max, negate=True)
        p = tile("p", [P, I], F32)
        z = tile("z", [P, 1], F32)
        nc.scalar.activation(p[:], a[:], ACT.Exp, bias=neg_max[:], accum_out=z[:])
        gout_codes, gout_scales = quantize("gout", gout_bf, gout_words)
        hs1_q.append(
            quantize("hs1_third", hs1_third[:].rearrange("p n t -> p (n t)"), tile("hs1_third_codes", [P, CHUNK], U32))
        )
        hs1_q.append(quantize("hs1_last", hs1_last, tile("hs1_last_codes", [P, CHUNK], U32, tag="keys_codes")))

        c0 = psum.tile([P, I], F32, name="c0")
        first = 0
        for codes, scales in hs1_q:
            width = codes.shape[1]
            product(c0[:, first : first + width], gout_codes[:], gout_scales[:], codes[:], scales[:])
            first += width

        over_z = tile("over_z", [P, 1], F32)
        nc.vector.reciprocal(over_z[:], z[:])
        row = tile("row", [P, 2], F32)
        nc.vector.tensor_scalar(row[:], factors[:], over_z[:], None, ALU.mult)

        direct = tile("direct", [P, I], F32)
        total = tile("total", [P, 1], F32)
        nc.vector.scalar_tensor_tensor(direct[:], c0[:], row[:, 0:1], p[:], ALU.mult, ALU.mult, accum_out=total[:])
        through_z = tile("through_z", [P, I], F32)
        nc.vector.tensor_scalar(through_z[:], p[:], total[:], row[:, 1:2], ALU.mult, ALU.mult)
        nc.vector.tensor_tensor(window[:].indirect(offsets[:]), direct[:], through_z[:], ALU.add)

        first = 0
        for width in STORE_WIDTHS:
            cols = slice(first, first + width)
            nc.vector.tensor_tensor(old_sb[:, cols], window[:, cols], old_sb[:, cols], ALU.add)
            nc.sync.dma_start(out[:, cols], old_sb[:, cols])
            first += width
